import numpy as np
import ml_dtypes


def mxq(x, axis, fmt="e4m3"):
    dtype, down = {"e4m3": (ml_dtypes.float8_e4m3fn, 7), "e5m2": (ml_dtypes.float8_e5m2, 14)}[fmt]
    v = np.moveaxis(np.asarray(x, np.float32).astype(ml_dtypes.bfloat16).astype(np.float64), axis, -1)
    blocks = v.reshape(v.shape[:-1] + (-1, 32))
    amax = np.abs(blocks).max(-1, keepdims=True)
    byte = np.maximum(np.where(amax > 0, np.frexp(amax)[1] - 1 + 127, 0) - down, 1)
    scale = np.exp2(byte - 127.0)
    codes = (blocks / scale).astype(np.float32).astype(dtype).astype(np.float64)
    return np.moveaxis((codes * scale).reshape(v.shape), -1, axis)


WIDE = False


def mx_kscale(k):
    if not WIDE:
        return np.ones(k)
    levels = np.array([10, -10, 5, -5, 0])
    if k % 512:
        return np.exp2(np.random.permutation(np.resize(levels, k // 32))).repeat(32)
    a = np.empty((k // 512, 16))
    for p in range(k // 512):
        a[p, :8] = np.random.permutation(np.resize(levels, 8))
        for g in range(8):
            far = levels[np.abs(levels - a[p, g]) >= 10]
            a[p, g + 8] = far[np.random.randint(len(far))]
    return np.exp2(a.ravel()).repeat(32)


def f64(x):
    return np.asarray(x).astype(np.float64)


def striped(idx):
    return np.tile(idx.reshape(-1, 16).T, (8, 1)).astype(np.uint16)


def unstriped(offs):
    return offs[:16].T.reshape(-1).astype(np.int64)


def pack_weight(w):
    k, n = w.shape
    w = f64(np.asarray(w, np.float32).astype(ml_dtypes.bfloat16)).reshape(k // 32, 32, n)
    amax = np.abs(w).max(1)
    byte = np.clip(np.where(amax > 0, np.frexp(amax)[1] - 1 + 127 - 7, 1), 1, 254)
    scaled = (w * np.exp2(127.0 - byte)[:, None, :]).reshape(k, n).astype(np.float32)
    words = np.ascontiguousarray(scaled.reshape(k // 512, 128, 4, n).transpose(0, 1, 3, 2)).astype(ml_dtypes.float8_e4m3fn).view(np.uint8)
    return words, np.ascontiguousarray(byte.astype(np.uint8).reshape(k // 512, 16, n))


def unpack_weight(words, scales):
    g, p, n, _ = words.shape
    vals = np.ascontiguousarray(words).view(ml_dtypes.float8_e4m3fn).astype(np.float64) * np.repeat(np.exp2(scales.astype(np.float64) - 127.0), 8, axis=1)[..., None]
    return vals.transpose(0, 1, 3, 2).reshape(g * 512, n)


def relu(v):
    return np.maximum(v, 0.0)


K, T, S, V, H, N, J = 1024, 2048, 1024, 512, 512, 128, 512


def setup_inputs():
    n = np.random.standard_normal
    s = mx_kscale(K)[:, None]
    u = mx_kscale(H)
    r = mx_kscale(J)[:, None]
    packed_xT = pack_weight(n((K, T)) * s)
    packed_w4 = pack_weight(n((H, N)) / np.sqrt(H) / u[:, None])
    return {
        "x_words": packed_xT[0],
        "x_scales": packed_xT[1],
        "eT": (n((J, V)) * r).astype(np.float32),
        "w1": (n((K, H)) / np.sqrt(3 * K) / s * u).astype(np.float32),
        "w2": (n((K, H)) / np.sqrt(3 * K) / s * u).astype(np.float32),
        "w3": (n((J, H)) / np.sqrt(3 * J) / r * u).astype(np.float32),
        "w4_words": packed_w4[0],
        "w4_scales": packed_w4[1],
        "offs": striped(np.random.permutation(T)[:S]),
    }


def reference(x_words, x_scales, eT, w1, w2, w3, w4_words, w4_scales, offs):
    xq = unpack_weight(x_words, x_scales)[:, unstriped(offs)]
    h = relu(mxq(f64(w1), 0, "e4m3").T @ xq[:, :V] + mxq(f64(w2), 0, "e4m3").T @ xq[:, V:2 * V] + mxq(f64(w3), 0, "e4m3").T @ mxq(f64(eT), 0, "e4m3"))
    return unpack_weight(w4_words, w4_scales).T @ mxq(h, 0, "e4m3")

@@ -1,0 +1,165 @@
+from contextlib import ExitStack
+
+import concourse.mybir as mybir
+from concourse.masks import make_identity
+
+K, T, S, V, H, N, J = 1024, 2048, 1024, 512, 512, 128, 512
+FLOPS = 2 * V * H * (2 * K + J) + 2 * V * H * N
+
+F32 = mybir.dt.float32
+BF16 = mybir.dt.bfloat16
+I32 = mybir.dt.int32
+U32 = mybir.dt.uint32
+U16 = mybir.dt.uint16
+U8 = mybir.dt.uint8
+FP8X4 = mybir.dt.float8_e4m3fn_x4
+RELU = mybir.ActivationFunctionType.Relu
+
+P = 128
+PACK = 4
+K_PASS = P * PACK
+CHUNK = 128
+CHUNKS = V // CHUNK
+
+
+def interleave(copy, grouped, raw):
+    copy(out=grouped.rearrange("p (c i) t -> p c t i", i=4), in_=raw.rearrange("p t (c i) -> p c t i", i=4))
+
+
+def quantize(nc, codes, scales, grouped):
+    nc.vector.quantize_mx(out=codes.bitcast(FP8X4), scales=scales, in_=grouped.rearrange("p c t -> p (c t)"))
+
+
+def tile_picked_edgeup_relu_p_kernel(
+    tc, x_words, x_scales, eT, w1, w2, w3, w4_words, w4_scales, offs, out
+):
+    nc = tc.nc
+    with ExitStack() as ctx:
+        keep = ctx.enter_context(tc.tile_pool(name="keep", bufs=1))
+        psum = ctx.enter_context(tc.psum_pool(name="psum", bufs=1))
+        psum2 = ctx.enter_context(tc.psum_pool(name="psum2", bufs=2))
+
+        def tile(name, shape, dtype):
+            return keep.tile(shape, dtype, name=name, align_bytes=64)
+
+        offsets = keep.tile([P, S // 16], U16, name="offsets")
+        node_words = [tile("node_words%d" % z, [P, T], U32) for z in range(2)]
+        node_scales = tile("node_scales", [P, T], U8)
+        end_words = [tile("end_words%d" % z, [P, S], U32) for z in range(2)]
+        end_scales = tile("end_scales", [P, S], U8)
+        w4_codes = tile("w4_codes", [P, N], U32)
+        w4_plane = tile("w4_plane", [P, N], U8)
+        ident = tile("ident", [P, P], F32)
+
+        nc.vector.memset(node_scales[:].bitcast(I32), 0)
+        nc.vector.memset(w4_plane[:].bitcast(I32), 0)
+        for q in range(4):
+            nc.gpsimd.dma_start(
+                out=node_scales[32 * q : 32 * q + 8, :].bitcast(I32), in_=x_scales[:, 4 * q : 4 * q + 4, :].bitcast(I32)
+            )
+        for q in range(4):
+            nc.gpsimd.dma_start(
+                out=w4_plane[32 * q : 32 * q + 4, :].bitcast(I32), in_=w4_scales[0, 4 * q : 4 * q + 4, :].bitcast(I32)
+            )
+        make_identity(nc, ident[:])
+
+        def load_words(dst, src):
+            nc.sync.dma_start(out=dst[:].bitcast(I32), in_=src.rearrange("p n t -> p (n t)").bitcast(I32))
+
+        def load_rows(name, rows, c0, c1):
+            raw = tile(name, [P, PACK, c1 - c0], F32)
+            nc.sync.dma_start(out=raw[:], in_=rows.rearrange("(p j) c -> p j c", j=PACK)[:, :, c0:c1])
+            return raw
+
+        load_words(node_words[0], x_words[0])
+        nc.sync.dma_start(offsets[:], offs)
+        raw_w = {}
+        raw_w[0, 0] = load_rows("raw_w00", w1[0:K_PASS, :], 0, H)
+        load_words(node_words[1], x_words[1])
+        raw_w[0, 1] = load_rows("raw_w01", w1[K_PASS:K, :], 0, H)
+        load_words(w4_codes, w4_words[0])
+        raw_w[1, 0] = load_rows("raw_w10", w2[0:K_PASS, :], 0, H)
+        raw_w[1, 1] = load_rows("raw_w11", w2[K_PASS:K, :], 0, H)
+        raw_w3 = [load_rows("raw_w3%d" % u, w3, u * 256, (u + 1) * 256) for u in range(2)]
+        raw_e = [load_rows("raw_e%d" % c, eT, c * CHUNK, (c + 1) * CHUNK) for c in range(CHUNKS)]
+
+        nc.vector.tensor_copy(end_words[0][:], node_words[0][:].indirect(offsets[:]))
+        nc.vector.tensor_copy(end_scales[:], node_scales[:].indirect(offsets[:]))
+        nc.vector.tensor_copy(end_words[1][:], node_words[1][:].indirect(offsets[:]))
+
+        hT = [psum.tile([P, H], F32, name="hT%d" % c) for c in range(CHUNKS)]
+
+        order = [(0, 0), (0, 1), (1, 0), (1, 1)]
+        for n, (side, z) in enumerate(order):
+            grouped = tile("w_bf%d" % n, [P, H, PACK], BF16)
+            codes = tile("w_codes%d" % n, [P, H], U32)
+            plane = tile("w_plane%d" % n, [P, H], U8)
+            interleave(nc.vector.tensor_copy if n == 3 else nc.scalar.copy, grouped[:], raw_w[side, z][:])
+            quantize(nc, codes[:], plane[:], grouped[:])
+            for c in range(CHUNKS):
+                cols = slice(side * V + c * CHUNK, side * V + (c + 1) * CHUNK)
+                nc.tensor.matmul_mx(
+                    out=hT[c][:],
+                    lhsT=end_words[z][:, cols].bitcast(FP8X4),
+                    lhsT_scale=end_scales[4 * z : P, cols],
+                    rhs=codes[:].bitcast(FP8X4),
+                    rhs_scale=plane[:],
+                    start=(n == 0),
+                    stop=False,
+                )
+
+        w3_codes = tile("w3_codes", [P, H], U32)
+        w3_plane = tile("w3_plane", [P, H], U8)
+        w3_bf = [tile("w3_bf%d" % u, [P, 256, PACK], BF16) for u in range(2)]
+        interleave(nc.scalar.copy, w3_bf[0][:], raw_w3[0][:])
+        quantize(nc, w3_codes[:, 0:256], w3_plane[:, 0:256], w3_bf[0][:])
+        interleave(nc.scalar.copy, w3_bf[1][:, 0:96, :], raw_w3[1][:, :, 0:96])
+        interleave(nc.vector.tensor_copy, w3_bf[1][:, 96:256, :], raw_w3[1][:, :, 96:256])
+        quantize(nc, w3_codes[:, 256:512], w3_plane[:, 256:512], w3_bf[1][:])
+
+        for c in range(CHUNKS):
+            e_bf = tile("e_bf%d" % c, [P, CHUNK, PACK], BF16)
+            e_codes = tile("e_codes%d" % c, [P, CHUNK], U32)
+            e_plane = tile("e_plane%d" % c, [P, CHUNK], U8)
+            interleave(nc.scalar.copy if c == 0 else nc.vector.tensor_copy, e_bf[:], raw_e[c][:])
+            quantize(nc, e_codes[:], e_plane[:], e_bf[:])
+            nc.tensor.matmul_mx(
+                out=hT[c][:],
+                lhsT=e_codes[:].bitcast(FP8X4),
+                lhsT_scale=e_plane[:],
+                rhs=w3_codes[:].bitcast(FP8X4),
+                rhs_scale=w3_plane[:],
+                start=False,
+                stop=True,
+            )
+            hT_bf = tile("hT_bf%d" % c, [P, H], BF16)
+            nc.scalar.activation(
+                out=hT_bf[:].rearrange("v (u p e) -> v u p e", u=2, e=2),
+                in_=hT[c][:].rearrange("v (p u e) -> v u p e", u=2, e=2),
+                func=RELU,
+            )
+            pairs = hT_bf[:].bitcast(F32)
+            turned = psum2.tile([P, 2, CHUNK], F32, name="turned")
+            for u in range(2):
+                nc.tensor.transpose(turned[:, u, :], pairs[:, u * P : (u + 1) * P], ident[:])
+            h_bf = tile("h_bf%d" % c, [P, CHUNK, PACK], BF16)
+            nc.vector.tensor_copy(
+                out=h_bf[:].rearrange("p v t -> p (v t)").bitcast(F32).rearrange("p (v u) -> p v u", u=2),
+                in_=turned[:].rearrange("p u v -> p v u"),
+            )
+            h_codes = tile("h_codes%d" % c, [P, CHUNK], U32)
+            h_plane = tile("h_plane%d" % c, [P, CHUNK], U8)
+            quantize(nc, h_codes[:], h_plane[:], h_bf[:])
+            acc = psum2.tile([P, CHUNK], F32, name="acc")
+            nc.tensor.matmul_mx(
+                out=acc[:],
+                lhsT=w4_codes[:].bitcast(FP8X4),
+                lhsT_scale=w4_plane[:],
+                rhs=h_codes[:].bitcast(FP8X4),
+                rhs_scale=h_plane[:],
+                start=True,
+                stop=True,
+            )
+            result = tile("result%d" % c, [P, CHUNK], F32)
+            nc.scalar.copy(out=result[:], in_=acc[:])
+            nc.sync.dma_start(out=out[:, c * CHUNK : (c + 1) * CHUNK], in_=result[:])

@@ -1,7 +1,6 @@
 from contextlib import ExitStack
 
 import concourse.mybir as mybir
-from concourse.masks import make_identity
 
 K, T, S, V, H, N, J = 1024, 2048, 1024, 512, 512, 128, 512
 FLOPS = 2 * V * H * (2 * K + J) + 2 * V * H * N
@@ -22,12 +21,8 @@ CHUNK = 128
 CHUNKS = V // CHUNK
 
 
-def interleave(copy, grouped, raw):
-    copy(out=grouped.rearrange("p (c i) t -> p c t i", i=4), in_=raw.rearrange("p t (c i) -> p c t i", i=4))
-
-
 def quantize(nc, codes, scales, grouped):
-    nc.vector.quantize_mx(out=codes.bitcast(FP8X4), scales=scales, in_=grouped.rearrange("p c t -> p (c t)"))
+    nc.vector.quantize_mx(out=codes.bitcast(FP8X4), scales=scales, in_=grouped)
 
 
 def tile_picked_edgeup_relu_p_kernel(
@@ -36,32 +31,32 @@ def tile_picked_edgeup_relu_p_kernel(
     nc = tc.nc
     with ExitStack() as ctx:
         keep = ctx.enter_context(tc.tile_pool(name="keep", bufs=1))
+        chain = ctx.enter_context(tc.tile_pool(name="chain", bufs=1))
         psum = ctx.enter_context(tc.psum_pool(name="psum", bufs=1))
-        psum2 = ctx.enter_context(tc.psum_pool(name="psum2", bufs=2))
 
         def tile(name, shape, dtype):
             return keep.tile(shape, dtype, name=name, align_bytes=64)
 
+        def placed(name, shape, dtype, offset):
+            return chain.tile(shape, dtype, name=name, align_bytes=64, offset=offset)
+
+        at_words0, at_scales, at_words1 = 0, 4 * T, 4 * T + 4 * S
         offsets = keep.tile([P, S // 16], U16, name="offsets")
-        node_words = [tile("node_words%d" % z, [P, T], U32) for z in range(2)]
-        node_scales = tile("node_scales", [P, T], U8)
-        end_words = [tile("end_words%d" % z, [P, S], U32) for z in range(2)]
-        end_scales = tile("end_scales", [P, S], U8)
+        node_words = [placed("node_words0", [P, T], U32, at_words0), placed("node_words1", [P, T], U32, at_words1)]
+        node_scales = placed("node_scales", [P, T], U8, at_scales)
         w4_codes = tile("w4_codes", [P, N], U32)
         w4_plane = tile("w4_plane", [P, N], U8)
-        ident = tile("ident", [P, P], F32)
 
-        nc.vector.memset(node_scales[:].bitcast(I32), 0)
-        nc.vector.memset(w4_plane[:].bitcast(I32), 0)
+        nc.gpsimd.memset(node_scales[:].bitcast(I32), 0)
         for q in range(4):
             nc.gpsimd.dma_start(
                 out=node_scales[32 * q : 32 * q + 8, :].bitcast(I32), in_=x_scales[:, 4 * q : 4 * q + 4, :].bitcast(I32)
             )
+        nc.vector.memset(w4_plane[:].bitcast(I32), 0)
         for q in range(4):
             nc.gpsimd.dma_start(
                 out=w4_plane[32 * q : 32 * q + 4, :].bitcast(I32), in_=w4_scales[0, 4 * q : 4 * q + 4, :].bitcast(I32)
             )
-        make_identity(nc, ident[:])
 
         def load_words(dst, src):
             nc.sync.dma_start(out=dst[:].bitcast(I32), in_=src.rearrange("p n t -> p (n t)").bitcast(I32))
@@ -73,84 +68,82 @@ def tile_picked_edgeup_relu_p_kernel(
 
         load_words(node_words[0], x_words[0])
         nc.sync.dma_start(offsets[:], offs)
-        raw_w = {}
-        raw_w[0, 0] = load_rows("raw_w00", w1[0:K_PASS, :], 0, H)
+        raw_w = [load_rows("raw_w0", w1[0:K_PASS, :], 0, H)]
         load_words(node_words[1], x_words[1])
-        raw_w[0, 1] = load_rows("raw_w01", w1[K_PASS:K, :], 0, H)
-        load_words(w4_codes, w4_words[0])
-        raw_w[1, 0] = load_rows("raw_w10", w2[0:K_PASS, :], 0, H)
-        raw_w[1, 1] = load_rows("raw_w11", w2[K_PASS:K, :], 0, H)
-        raw_w3 = [load_rows("raw_w3%d" % u, w3, u * 256, (u + 1) * 256) for u in range(2)]
+        raw_w.append(load_rows("raw_w1", w1[K_PASS:K, :], 0, H))
+        raw_w.append(load_rows("raw_w2", w2[0:K_PASS, :], 0, H))
+        raw_w.append(load_rows("raw_w3", w2[K_PASS:K, :], 0, H))
+        raw_w.append(load_rows("raw_w4", w3, 0, H))
         raw_e = [load_rows("raw_e%d" % c, eT, c * CHUNK, (c + 1) * CHUNK) for c in range(CHUNKS)]
+        load_words(w4_codes, w4_words[0])
 
+        end_words = [tile("end_words0", [P, S], U32), placed("end_words1", [P, S], U32, at_scales)]
+        end_scales = placed("end_scales", [P, S], U8, at_words0)
         nc.vector.tensor_copy(end_words[0][:], node_words[0][:].indirect(offsets[:]))
         nc.vector.tensor_copy(end_scales[:], node_scales[:].indirect(offsets[:]))
         nc.vector.tensor_copy(end_words[1][:], node_words[1][:].indirect(offsets[:]))
 
-        hT = [psum.tile([P, H], F32, name="hT%d" % c) for c in range(CHUNKS)]
+        hidden = [psum.tile([P, PACK, CHUNK], F32, name="hidden%d" % c) for c in range(CHUNKS)]
 
-        order = [(0, 0), (0, 1), (1, 0), (1, 1)]
-        for n, (side, z) in enumerate(order):
-            grouped = tile("w_bf%d" % n, [P, H, PACK], BF16)
-            codes = tile("w_codes%d" % n, [P, H], U32)
-            plane = tile("w_plane%d" % n, [P, H], U8)
-            interleave(nc.vector.tensor_copy if n == 3 else nc.scalar.copy, grouped[:], raw_w[side, z][:])
-            quantize(nc, codes[:], plane[:], grouped[:])
-            for c in range(CHUNKS):
-                cols = slice(side * V + c * CHUNK, side * V + (c + 1) * CHUNK)
-                nc.tensor.matmul_mx(
-                    out=hT[c][:],
-                    lhsT=end_words[z][:, cols].bitcast(FP8X4),
-                    lhsT_scale=end_scales[4 * z : P, cols],
-                    rhs=codes[:].bitcast(FP8X4),
-                    rhs_scale=plane[:],
-                    start=(n == 0),
-                    stop=False,
-                )
+        def weight_half(n, u, copy):
+            grouped = tile("w_bf%d_%d" % (n, u), [P, 2, P, PACK], BF16)
+            if n == 0:
+                codes = placed("w_codes%d_%d" % (n, u), [P, 2 * P], U32, at_words1 + u * 8 * P)
+            else:
+                codes = tile("w_codes%d_%d" % (n, u), [P, 2 * P], U32)
+            plane = tile("w_plane%d_%d" % (n, u), [P, 2 * P], U8)
+            copy(
+                out=grouped[:].rearrange("p t m j -> p m j t"),
+                in_=raw_w[n][:].rearrange("p j (m t) -> p m j t", t=PACK)[:, :, :, 2 * u : 2 * u + 2],
+            )
+            quantize(nc, codes[:], plane[:], grouped[:].rearrange("p t m j -> p (t m j)"))
+            return codes, plane
 
-        w3_codes = tile("w3_codes", [P, H], U32)
-        w3_plane = tile("w3_plane", [P, H], U8)
-        w3_bf = [tile("w3_bf%d" % u, [P, 256, PACK], BF16) for u in range(2)]
-        interleave(nc.scalar.copy, w3_bf[0][:], raw_w3[0][:])
-        quantize(nc, w3_codes[:, 0:256], w3_plane[:, 0:256], w3_bf[0][:])
-        interleave(nc.scalar.copy, w3_bf[1][:, 0:96, :], raw_w3[1][:, :, 0:96])
-        interleave(nc.vector.tensor_copy, w3_bf[1][:, 96:256, :], raw_w3[1][:, :, 96:256])
-        quantize(nc, w3_codes[:, 256:512], w3_plane[:, 256:512], w3_bf[1][:])
+        def multiply(c, t, codes, plane, words, scales, start, stop):
+            cols = slice((t % 2) * P, (t % 2 + 1) * P)
+            nc.tensor.matmul_mx(
+                out=hidden[c][:, t, :],
+                lhsT=codes[:, cols].bitcast(FP8X4),
+                lhsT_scale=plane[:, cols],
+                rhs=words.bitcast(FP8X4),
+                rhs_scale=scales,
+                start=start,
+                stop=stop,
+            )
+
+        for n in range(4):
+            side, z = divmod(n, 2)
+            for u in range(2):
+                copy = nc.vector.tensor_copy if (n >= 2 and u == 0) else nc.scalar.copy
+                codes, plane = weight_half(n, u, copy)
+                for t in (2 * u, 2 * u + 1):
+                    for c in range(CHUNKS):
+                        cols = slice(side * V + c * CHUNK, side * V + (c + 1) * CHUNK)
+                        multiply(
+                            c, t, codes, plane, end_words[z][:, cols], end_scales[4 * z : P, cols], n == 0 and t == 0, False
+                        )
+
+        w3_halves = [weight_half(4, 0, nc.vector.tensor_copy), weight_half(4, 1, nc.scalar.copy)]
 
         for c in range(CHUNKS):
             e_bf = tile("e_bf%d" % c, [P, CHUNK, PACK], BF16)
             e_codes = tile("e_codes%d" % c, [P, CHUNK], U32)
             e_plane = tile("e_plane%d" % c, [P, CHUNK], U8)
-            interleave(nc.scalar.copy if c == 0 else nc.vector.tensor_copy, e_bf[:], raw_e[c][:])
-            quantize(nc, e_codes[:], e_plane[:], e_bf[:])
-            nc.tensor.matmul_mx(
-                out=hT[c][:],
-                lhsT=e_codes[:].bitcast(FP8X4),
-                lhsT_scale=e_plane[:],
-                rhs=w3_codes[:].bitcast(FP8X4),
-                rhs_scale=w3_plane[:],
-                start=False,
-                stop=True,
+            copy = nc.scalar.copy if c == 0 else nc.vector.tensor_copy
+            copy(
+                out=e_bf[:].rearrange("p (c i) j -> p c j i", i=4),
+                in_=raw_e[c][:].rearrange("p j (c i) -> p c j i", i=4),
             )
-            hT_bf = tile("hT_bf%d" % c, [P, H], BF16)
-            nc.scalar.activation(
-                out=hT_bf[:].rearrange("v (u p e) -> v u p e", u=2, e=2),
-                in_=hT[c][:].rearrange("v (p u e) -> v u p e", u=2, e=2),
-                func=RELU,
-            )
-            pairs = hT_bf[:].bitcast(F32)
-            turned = psum2.tile([P, 2, CHUNK], F32, name="turned")
-            for u in range(2):
-                nc.tensor.transpose(turned[:, u, :], pairs[:, u * P : (u + 1) * P], ident[:])
+            quantize(nc, e_codes[:], e_plane[:], e_bf[:].rearrange("p c j -> p (c j)"))
+            for t in range(PACK):
+                codes, plane = w3_halves[t // 2]
+                multiply(c, t, codes, plane, e_codes[:], e_plane[:], False, t == PACK - 1)
             h_bf = tile("h_bf%d" % c, [P, CHUNK, PACK], BF16)
-            nc.vector.tensor_copy(
-                out=h_bf[:].rearrange("p v t -> p (v t)").bitcast(F32).rearrange("p (v u) -> p v u", u=2),
-                in_=turned[:].rearrange("p u v -> p v u"),
-            )
+            nc.scalar.activation(out=h_bf[:], in_=hidden[c][:].rearrange("p t v -> p v t"), func=RELU)
             h_codes = tile("h_codes%d" % c, [P, CHUNK], U32)
             h_plane = tile("h_plane%d" % c, [P, CHUNK], U8)
-            quantize(nc, h_codes[:], h_plane[:], h_bf[:])
-            acc = psum2.tile([P, CHUNK], F32, name="acc")
+            quantize(nc, h_codes[:], h_plane[:], h_bf[:].rearrange("p v t -> p (v t)"))
+            acc = psum.tile([P, CHUNK], F32, name="acc%d" % c)
             nc.tensor.matmul_mx(
                 out=acc[:],
                 lhsT=w4_codes[:].bitcast(FP8X4),

@@ -40,23 +40,19 @@ def tile_picked_edgeup_relu_p_kernel(
         def placed(name, shape, dtype, offset):
             return chain.tile(shape, dtype, name=name, align_bytes=64, offset=offset)
 
-        at_words0, at_scales, at_words1 = 0, 4 * T, 4 * T + 4 * S
+        at_words0, at_words1, at_scales = 0, 4 * T, 8 * T
         offsets = keep.tile([P, S // 16], U16, name="offsets")
         node_words = [placed("node_words0", [P, T], U32, at_words0), placed("node_words1", [P, T], U32, at_words1)]
         node_scales = placed("node_scales", [P, T], U8, at_scales)
         w4_codes = tile("w4_codes", [P, N], U32)
         w4_plane = tile("w4_plane", [P, N], U8)
 
-        nc.gpsimd.memset(node_scales[:].bitcast(I32), 0)
-        for q in range(4):
+        nc.vector.memset(node_scales[:].bitcast(I32), 0)
+        for q in range(2, 4):
             nc.gpsimd.dma_start(
                 out=node_scales[32 * q : 32 * q + 8, :].bitcast(I32), in_=x_scales[:, 4 * q : 4 * q + 4, :].bitcast(I32)
             )
         nc.vector.memset(w4_plane[:].bitcast(I32), 0)
-        for q in range(4):
-            nc.gpsimd.dma_start(
-                out=w4_plane[32 * q : 32 * q + 4, :].bitcast(I32), in_=w4_scales[0, 4 * q : 4 * q + 4, :].bitcast(I32)
-            )
 
         def load_words(dst, src):
             nc.sync.dma_start(out=dst[:].bitcast(I32), in_=src.rearrange("p n t -> p (n t)").bitcast(I32))
@@ -67,28 +63,37 @@ def tile_picked_edgeup_relu_p_kernel(
             return raw
 
         load_words(node_words[0], x_words[0])
+        for q in range(2):
+            nc.sync.dma_start(
+                out=node_scales[32 * q : 32 * q + 8, :].bitcast(I32), in_=x_scales[:, 4 * q : 4 * q + 4, :].bitcast(I32)
+            )
         nc.sync.dma_start(offsets[:], offs)
         raw_w = [load_rows("raw_w0", w1[0:K_PASS, :], 0, H)]
+        raw_w.append(load_rows("raw_w1", w2[0:K_PASS, :], 0, H))
         load_words(node_words[1], x_words[1])
-        raw_w.append(load_rows("raw_w1", w1[K_PASS:K, :], 0, H))
-        raw_w.append(load_rows("raw_w2", w2[0:K_PASS, :], 0, H))
+        raw_w.append(load_rows("raw_w2", w1[K_PASS:K, :], 0, H))
         raw_w.append(load_rows("raw_w3", w2[K_PASS:K, :], 0, H))
         raw_w.append(load_rows("raw_w4", w3, 0, H))
-        raw_e = [load_rows("raw_e%d" % c, eT, c * CHUNK, (c + 1) * CHUNK) for c in range(CHUNKS)]
+        first = load_rows("raw_e01", eT, 0, 2 * CHUNK)
+        raw_e = [first[:, :, 0:CHUNK], first[:, :, CHUNK : 2 * CHUNK]]
+        raw_e.extend(load_rows("raw_e%d" % c, eT, c * CHUNK, (c + 1) * CHUNK)[:] for c in range(2, CHUNKS))
         load_words(w4_codes, w4_words[0])
+        for q in range(4):
+            nc.sync.dma_start(
+                out=w4_plane[32 * q : 32 * q + 4, :].bitcast(I32), in_=w4_scales[0, 4 * q : 4 * q + 4, :].bitcast(I32)
+            )
 
-        end_words = [tile("end_words0", [P, S], U32), placed("end_words1", [P, S], U32, at_scales)]
+        end_words = [tile("end_words0", [P, S], U32), tile("end_words1", [P, S], U32)]
         end_scales = placed("end_scales", [P, S], U8, at_words0)
         nc.vector.tensor_copy(end_words[0][:], node_words[0][:].indirect(offsets[:]))
         nc.vector.tensor_copy(end_scales[:], node_scales[:].indirect(offsets[:]))
-        nc.vector.tensor_copy(end_words[1][:], node_words[1][:].indirect(offsets[:]))
 
         hidden = [psum.tile([P, PACK, CHUNK], F32, name="hidden%d" % c) for c in range(CHUNKS)]
 
         def weight_half(n, u, copy):
             grouped = tile("w_bf%d_%d" % (n, u), [P, 2, P, PACK], BF16)
             if n == 0:
-                codes = placed("w_codes%d_%d" % (n, u), [P, 2 * P], U32, at_words1 + u * 8 * P)
+                codes = placed("w_codes%d_%d" % (n, u), [P, 2 * P], U32, at_scales + u * 8 * P)
             else:
                 codes = tile("w_codes%d_%d" % (n, u), [P, 2 * P], U32)
             plane = tile("w_plane%d_%d" % (n, u), [P, 2 * P], U8)
@@ -112,9 +117,11 @@ def tile_picked_edgeup_relu_p_kernel(
             )
 
         for n in range(4):
-            side, z = divmod(n, 2)
+            z, side = divmod(n, 2)
+            if n == 2:
+                nc.vector.tensor_copy(end_words[1][:], node_words[1][:].indirect(offsets[:]))
             for u in range(2):
-                copy = nc.vector.tensor_copy if (n >= 2 and u == 0) else nc.scalar.copy
+                copy = nc.vector.tensor_copy if (n == 3 and u == 0) else nc.scalar.copy
                 codes, plane = weight_half(n, u, copy)
                 for t in (2 * u, 2 * u + 1):
                     for c in range(CHUNKS):
@@ -129,23 +136,27 @@ def tile_picked_edgeup_relu_p_kernel(
             e_bf = tile("e_bf%d" % c, [P, CHUNK, PACK], BF16)
             e_codes = tile("e_codes%d" % c, [P, CHUNK], U32)
             e_plane = tile("e_plane%d" % c, [P, CHUNK], U8)
-            copy = nc.scalar.copy if c == 0 else nc.vector.tensor_copy
+            copy = nc.scalar.copy if c < 2 else nc.vector.tensor_copy
             copy(
                 out=e_bf[:].rearrange("p (c i) j -> p c j i", i=4),
-                in_=raw_e[c][:].rearrange("p j (c i) -> p c j i", i=4),
+                in_=raw_e[c].rearrange("p j (c i) -> p c j i", i=4),
             )
             quantize(nc, e_codes[:], e_plane[:], e_bf[:].rearrange("p c j -> p (c j)"))
             for t in range(PACK):
                 codes, plane = w3_halves[t // 2]
                 multiply(c, t, codes, plane, e_codes[:], e_plane[:], False, t == PACK - 1)
-            h_bf = tile("h_bf%d" % c, [P, CHUNK, PACK], BF16)
-            nc.scalar.activation(out=h_bf[:], in_=hidden[c][:].rearrange("p t v -> p v t"), func=RELU)
+
+        h_bf = [tile("h_bf%d" % c, [P, CHUNK, PACK], BF16) for c in range(CHUNKS)]
+        for c in range(CHUNKS):
+            nc.scalar.activation(out=h_bf[c][:], in_=hidden[c][:].rearrange("p t v -> p v t"), func=RELU)
+
+        acc = [psum.tile([P, CHUNK], F32, name="acc%d" % c) for c in range(CHUNKS)]
+        for c in range(CHUNKS):
             h_codes = tile("h_codes%d" % c, [P, CHUNK], U32)
             h_plane = tile("h_plane%d" % c, [P, CHUNK], U8)
-            quantize(nc, h_codes[:], h_plane[:], h_bf[:].rearrange("p v t -> p (v t)"))
-            acc = psum.tile([P, CHUNK], F32, name="acc%d" % c)
+            quantize(nc, h_codes[:], h_plane[:], h_bf[c][:].rearrange("p v t -> p (v t)"))
             nc.tensor.matmul_mx(
-                out=acc[:],
+                out=acc[c][:],
                 lhsT=w4_codes[:].bitcast(FP8X4),
                 lhsT_scale=w4_plane[:],
                 rhs=h_codes[:].bitcast(FP8X4),
@@ -153,6 +164,8 @@ def tile_picked_edgeup_relu_p_kernel(
                 start=True,
                 stop=True,
             )
+
+        for c in range(CHUNKS):
             result = tile("result%d" % c, [P, CHUNK], F32)
-            nc.scalar.copy(out=result[:], in_=acc[:])
+            nc.scalar.copy(out=result[:], in_=acc[c][:])
             nc.sync.dma_start(out=out[:, c * CHUNK : (c + 1) * CHUNK], in_=result[:])

@@ -17,12 +17,9 @@ RELU = mybir.ActivationFunctionType.Relu
 P = 128
 PACK = 4
 K_PASS = P * PACK
-CHUNK = 128
-CHUNKS = V // CHUNK
-
-
-def quantize(nc, codes, scales, grouped):
-    nc.vector.quantize_mx(out=codes.bitcast(FP8X4), scales=scales, in_=grouped)
+WIDTH = 128
+WINDOWS = [(0, 128), (128, 128), (256, 128), (384, 64), (448, 64)]
+PIECES = [(0, 256), (256, 384), (384, 512)]
 
 
 def tile_picked_edgeup_relu_p_kernel(
@@ -40,6 +37,20 @@ def tile_picked_edgeup_relu_p_kernel(
         def placed(name, shape, dtype, offset):
             return chain.tile(shape, dtype, name=name, align_bytes=64, offset=offset)
 
+        def quantize(codes, plane, rounded):
+            nc.vector.quantize_mx(out=codes.bitcast(FP8X4), scales=plane, in_=rounded)
+
+        def multiply(sums, still, still_plane, moving, moving_plane, start, stop):
+            nc.tensor.matmul_mx(
+                out=sums,
+                lhsT=still.bitcast(FP8X4),
+                lhsT_scale=still_plane,
+                rhs=moving.bitcast(FP8X4),
+                rhs_scale=moving_plane,
+                start=start,
+                stop=stop,
+            )
+
         at_words0, at_words1, at_scales = 0, 4 * T, 8 * T
         offsets = keep.tile([P, S // 16], U16, name="offsets")
         node_words = [placed("node_words0", [P, T], U32, at_words0), placed("node_words1", [P, T], U32, at_words1)]
@@ -47,36 +58,33 @@ def tile_picked_edgeup_relu_p_kernel(
         w4_codes = tile("w4_codes", [P, N], U32)
         w4_plane = tile("w4_plane", [P, N], U8)
 
-        nc.vector.memset(node_scales[:].bitcast(I32), 0)
-        for q in range(2, 4):
-            nc.gpsimd.dma_start(
+        def load_node_scales(queue, q):
+            queue.dma_start(
                 out=node_scales[32 * q : 32 * q + 8, :].bitcast(I32), in_=x_scales[:, 4 * q : 4 * q + 4, :].bitcast(I32)
             )
-        nc.vector.memset(w4_plane[:].bitcast(I32), 0)
 
-        def load_words(dst, src):
-            nc.sync.dma_start(out=dst[:].bitcast(I32), in_=src.rearrange("p n t -> p (n t)").bitcast(I32))
+        def load_words(dst, words):
+            nc.sync.dma_start(out=dst[:].bitcast(I32), in_=words.rearrange("p n t -> p (n t)").bitcast(I32))
 
         def load_rows(name, rows, c0, c1):
             raw = tile(name, [P, PACK, c1 - c0], F32)
             nc.sync.dma_start(out=raw[:], in_=rows.rearrange("(p j) c -> p j c", j=PACK)[:, :, c0:c1])
             return raw
 
+        nc.vector.memset(node_scales[:].bitcast(I32), 0)
+        for q in (0, 2, 3):
+            load_node_scales(nc.gpsimd, q)
+        nc.vector.memset(w4_plane[:].bitcast(I32), 0)
+
         load_words(node_words[0], x_words[0])
-        for q in range(2):
-            nc.sync.dma_start(
-                out=node_scales[32 * q : 32 * q + 8, :].bitcast(I32), in_=x_scales[:, 4 * q : 4 * q + 4, :].bitcast(I32)
-            )
+        load_node_scales(nc.sync, 1)
         nc.sync.dma_start(offsets[:], offs)
-        raw_w = [load_rows("raw_w0", w1[0:K_PASS, :], 0, H)]
-        raw_w.append(load_rows("raw_w1", w2[0:K_PASS, :], 0, H))
+        raw_w = [load_rows("raw_w0", w1[0:K_PASS, :], 0, H), load_rows("raw_w1", w2[0:K_PASS, :], 0, H)]
         load_words(node_words[1], x_words[1])
         raw_w.append(load_rows("raw_w2", w1[K_PASS:K, :], 0, H))
         raw_w.append(load_rows("raw_w3", w2[K_PASS:K, :], 0, H))
         raw_w.append(load_rows("raw_w4", w3, 0, H))
-        first = load_rows("raw_e01", eT, 0, 2 * CHUNK)
-        raw_e = [first[:, :, 0:CHUNK], first[:, :, CHUNK : 2 * CHUNK]]
-        raw_e.extend(load_rows("raw_e%d" % c, eT, c * CHUNK, (c + 1) * CHUNK)[:] for c in range(2, CHUNKS))
+        raw_e = [load_rows("raw_e%d" % n, eT, c0, c1) for n, (c0, c1) in enumerate(PIECES)]
         load_words(w4_codes, w4_words[0])
         for q in range(4):
             nc.sync.dma_start(
@@ -88,7 +96,7 @@ def tile_picked_edgeup_relu_p_kernel(
         nc.vector.tensor_copy(end_words[0][:], node_words[0][:].indirect(offsets[:]))
         nc.vector.tensor_copy(end_scales[:], node_scales[:].indirect(offsets[:]))
 
-        hidden = [psum.tile([P, PACK, CHUNK], F32, name="hidden%d" % c) for c in range(CHUNKS)]
+        hidden = [psum.tile([P, PACK, WIDTH], F32, name="hidden%d" % w) for w in range(len(WINDOWS))]
 
         def weight_half(n, u, copy):
             grouped = tile("w_bf%d_%d" % (n, u), [P, 2, P, PACK], BF16)
@@ -98,74 +106,92 @@ def tile_picked_edgeup_relu_p_kernel(
                 codes = tile("w_codes%d_%d" % (n, u), [P, 2 * P], U32)
             plane = tile("w_plane%d_%d" % (n, u), [P, 2 * P], U8)
             copy(
-                out=grouped[:].rearrange("p t m j -> p m j t"),
-                in_=raw_w[n][:].rearrange("p j (m t) -> p m j t", t=PACK)[:, :, :, 2 * u : 2 * u + 2],
+                out=grouped[:].rearrange("p t (a b) j -> p a j b t", b=2),
+                in_=raw_w[n][:].rearrange("p j (a b t) -> p a j b t", b=2, t=PACK)[:, :, :, :, 2 * u : 2 * u + 2],
             )
-            quantize(nc, codes[:], plane[:], grouped[:].rearrange("p t m j -> p (t m j)"))
+            quantize(codes[:], plane[:], grouped[:].rearrange("p t m j -> p (t m j)"))
             return codes, plane
 
-        def multiply(c, t, codes, plane, words, scales, start, stop):
+        def first_layer(w, t, half, words, scales, start, stop):
             cols = slice((t % 2) * P, (t % 2 + 1) * P)
-            nc.tensor.matmul_mx(
-                out=hidden[c][:, t, :],
-                lhsT=codes[:, cols].bitcast(FP8X4),
-                lhsT_scale=plane[:, cols],
-                rhs=words.bitcast(FP8X4),
-                rhs_scale=scales,
-                start=start,
-                stop=stop,
-            )
+            multiply(hidden[w][:, t, :], half[0][:, cols], half[1][:, cols], words, scales, start, stop)
 
         for n in range(4):
             z, side = divmod(n, 2)
             if n == 2:
                 nc.vector.tensor_copy(end_words[1][:], node_words[1][:].indirect(offsets[:]))
             for u in range(2):
-                copy = nc.vector.tensor_copy if (n == 3 and u == 0) else nc.scalar.copy
-                codes, plane = weight_half(n, u, copy)
+                half = weight_half(n, u, nc.vector.tensor_copy if (n == 3 and u == 0) else nc.scalar.copy)
                 for t in (2 * u, 2 * u + 1):
-                    for c in range(CHUNKS):
-                        cols = slice(side * V + c * CHUNK, side * V + (c + 1) * CHUNK)
-                        multiply(
-                            c, t, codes, plane, end_words[z][:, cols], end_scales[4 * z : P, cols], n == 0 and t == 0, False
-                        )
+                    for w, (v0, count) in enumerate(WINDOWS):
+                        cols = slice(side * V + v0 + count - WIDTH, side * V + v0 + count)
+                        first_layer(w, t, half, end_words[z][:, cols], end_scales[4 * z : P, cols], n == 0 and t == 0, False)
 
         w3_halves = [weight_half(4, 0, nc.vector.tensor_copy), weight_half(4, 1, nc.scalar.copy)]
 
-        for c in range(CHUNKS):
-            e_bf = tile("e_bf%d" % c, [P, CHUNK, PACK], BF16)
-            e_codes = tile("e_codes%d" % c, [P, CHUNK], U32)
-            e_plane = tile("e_plane%d" % c, [P, CHUNK], U8)
-            copy = nc.scalar.copy if c < 2 else nc.vector.tensor_copy
+        e_codes = {0: tile("e_codes0", [P, WIDTH], U32), 2: tile("e_codes2", [P, WIDTH], U32)}
+        e_plane = {0: tile("e_plane0", [P, WIDTH], U8), 2: tile("e_plane2", [P, WIDTH], U8)}
+        row_codes = tile("e_row_codes", [P, 2 * WIDTH], U32)
+        row_plane = tile("e_row_plane", [P, 2 * WIDTH], U8)
+        row_end = {1: 128, 3: 192, 4: 256}
+
+        def edge_columns(w, count):
+            if w in row_end:
+                cols = slice(row_end[w] - count, row_end[w])
+                return row_codes[:, cols], row_plane[:, cols]
+            return e_codes[w][:], e_plane[w][:]
+
+        def round_edges(w, copy):
+            v0, count = WINDOWS[w]
+            n = [c0 <= v0 < c1 for c0, c1 in PIECES].index(True)
+            at = v0 - PIECES[n][0]
+            e_bf = keep.tile([P, count, PACK], BF16, name="e_bf%d" % w, tag={3: "e_bf2", 4: "h_bf2"}.get(w, "e_bf%d" % w), align_bytes=64)
             copy(
                 out=e_bf[:].rearrange("p (c i) j -> p c j i", i=4),
-                in_=raw_e[c].rearrange("p j (c i) -> p c j i", i=4),
+                in_=raw_e[n][:, :, at : at + count].rearrange("p j (c i) -> p c j i", i=4),
             )
-            quantize(nc, e_codes[:], e_plane[:], e_bf[:].rearrange("p c j -> p (c j)"))
+            return e_bf
+
+        def close_window(w, e_bf):
+            quantize(*edge_columns(w, WINDOWS[w][1]), e_bf[:].rearrange("p c j -> p (c j)"))
             for t in range(PACK):
-                codes, plane = w3_halves[t // 2]
-                multiply(c, t, codes, plane, e_codes[:], e_plane[:], False, t == PACK - 1)
+                first_layer(w, t, w3_halves[t // 2], *edge_columns(w, WIDTH), False, t == PACK - 1)
 
-        h_bf = [tile("h_bf%d" % c, [P, CHUNK, PACK], BF16) for c in range(CHUNKS)]
-        for c in range(CHUNKS):
-            nc.scalar.activation(out=h_bf[c][:], in_=hidden[c][:].rearrange("p t v -> p v t"), func=RELU)
+        def relu(w, on_vector):
+            count = WINDOWS[w][1]
+            h_bf = tile("h_bf%d" % w, [P, count, PACK], BF16)
+            sums = hidden[w][:, :, WIDTH - count : WIDTH].rearrange("p t v -> p v t")
+            if on_vector:
+                nc.vector.tensor_scalar_max(h_bf[:], sums, 0.0)
+            else:
+                nc.scalar.activation(out=h_bf[:], in_=sums, func=RELU)
+            return h_bf
 
-        acc = [psum.tile([P, CHUNK], F32, name="acc%d" % c) for c in range(CHUNKS)]
-        for c in range(CHUNKS):
-            h_codes = tile("h_codes%d" % c, [P, CHUNK], U32)
-            h_plane = tile("h_plane%d" % c, [P, CHUNK], U8)
-            quantize(nc, h_codes[:], h_plane[:], h_bf[c][:].rearrange("p v t -> p (v t)"))
-            nc.tensor.matmul_mx(
-                out=acc[c][:],
-                lhsT=w4_codes[:].bitcast(FP8X4),
-                lhsT_scale=w4_plane[:],
-                rhs=h_codes[:].bitcast(FP8X4),
-                rhs_scale=h_plane[:],
-                start=True,
-                stop=True,
-            )
+        spare = [psum.tile([P, WIDTH], F32, name="acc%d" % n) for n in range(3)]
+        acc = [spare[0][:], spare[1][:], hidden[0][:, 0, :], spare[2][:, 0:64], hidden[1][:, 0, 0:64]]
+        results = [tile("result%d" % c, [P, WIDTH], F32) for c in range(V // WIDTH)]
 
-        for c in range(CHUNKS):
-            result = tile("result%d" % c, [P, CHUNK], F32)
-            nc.scalar.copy(out=result[:], in_=acc[c][:])
-            nc.sync.dma_start(out=out[:, c * CHUNK : (c + 1) * CHUNK], in_=result[:])
+        def second_layer(w, h_bf):
+            count = WINDOWS[w][1]
+            h_codes = tile("h_codes%d" % w, [P, count], U32)
+            h_plane = tile("h_plane%d" % w, [P, count], U8)
+            quantize(h_codes[:], h_plane[:], h_bf[:].rearrange("p v t -> p (v t)"))
+            multiply(acc[w], w4_codes[:], w4_plane[:], h_codes[:], h_plane[:], True, True)
+
+        def leave(w, copy):
+            v0, count = WINDOWS[w]
+            c, at = divmod(v0, WIDTH)
+            copy(out=results[c][:, at : at + count], in_=acc[w])
+            if at + count == WIDTH:
+                nc.sync.dma_start(out=out[:, c * WIDTH : (c + 1) * WIDTH], in_=results[c][:])
+
+        for w, copy in ((0, nc.scalar.copy), (1, nc.vector.tensor_copy), (2, nc.scalar.copy)):
+            close_window(w, round_edges(w, copy))
+        narrow = [round_edges(w, nc.vector.tensor_copy) for w in (3, 4)]
+        close_window(3, narrow[0])
+        close_window(4, narrow[1])
+        rounded = [relu(w, w == 2) for w in range(len(WINDOWS))]
+        for w in range(len(WINDOWS)):
+            second_layer(w, rounded[w])
+        for w in range(len(WINDOWS)):
+            leave(w, nc.scalar.copy if w < 3 else nc.vector.tensor_copy)

@@ -32,10 +32,10 @@ def tile_picked_edgeup_relu_p_kernel(
         psum = ctx.enter_context(tc.psum_pool(name="psum", bufs=1))
 
         def tile(name, shape, dtype):
-            return keep.tile(shape, dtype, name=name, align_bytes=64)
+            return keep.tile(shape, dtype, name=name, align_bytes=256)
 
         def placed(name, shape, dtype, offset):
-            return chain.tile(shape, dtype, name=name, align_bytes=64, offset=offset)
+            return chain.tile(shape, dtype, name=name, align_bytes=256, offset=offset)
 
         def quantize(codes, plane, rounded):
             nc.vector.quantize_mx(out=codes.bitcast(FP8X4), scales=plane, in_=rounded)
@@ -52,7 +52,7 @@ def tile_picked_edgeup_relu_p_kernel(
             )
 
         at_words0, at_words1, at_scales = 0, 4 * T, 8 * T
-        offsets = keep.tile([P, S // 16], U16, name="offsets")
+        offsets = keep.tile([P, S // 16], U16, name="offsets", align_bytes=256)
         node_words = [placed("node_words0", [P, T], U32, at_words0), placed("node_words1", [P, T], U32, at_words1)]
         node_scales = placed("node_scales", [P, T], U8, at_scales)
         w4_codes = tile("w4_codes", [P, N], U32)
@@ -145,7 +145,7 @@ def tile_picked_edgeup_relu_p_kernel(
             v0, count = WINDOWS[w]
             n = [c0 <= v0 < c1 for c0, c1 in PIECES].index(True)
             at = v0 - PIECES[n][0]
-            e_bf = keep.tile([P, count, PACK], BF16, name="e_bf%d" % w, tag={3: "e_bf2", 4: "h_bf2"}.get(w, "e_bf%d" % w), align_bytes=64)
+            e_bf = keep.tile([P, count, PACK], BF16, name="e_bf%d" % w, tag={3: "e_bf2", 4: "h_bf2"}.get(w, "e_bf%d" % w), align_bytes=256)
             copy(
                 out=e_bf[:].rearrange("p (c i) j -> p c j i", i=4),
                 in_=raw_e[n][:, :, at : at + count].rearrange("p j (c i) -> p c j i", i=4),

@@ -92,7 +92,7 @@ def tile_picked_edgeup_relu_p_kernel(
             )
 
         end_words = [tile("end_words0", [P, S], U32), tile("end_words1", [P, S], U32)]
-        end_scales = placed("end_scales", [P, S], U8, at_words0)
+        end_scales = tile("end_scales", [P, S], U8)
         nc.vector.tensor_copy(end_words[0][:], node_words[0][:].indirect(offsets[:]))
         nc.vector.tensor_copy(end_scales[:], node_scales[:].indirect(offsets[:]))
 
@@ -100,10 +100,7 @@ def tile_picked_edgeup_relu_p_kernel(
 
         def weight_half(n, u, copy):
             grouped = tile("w_bf%d_%d" % (n, u), [P, 2, P, PACK], BF16)
-            if n == 0:
-                codes = placed("w_codes%d_%d" % (n, u), [P, 2 * P], U32, at_scales + u * 8 * P)
-            else:
-                codes = tile("w_codes%d_%d" % (n, u), [P, 2 * P], U32)
+            codes = tile("w_codes%d_%d" % (n, u), [P, 2 * P], U32)
             plane = tile("w_plane%d_%d" % (n, u), [P, 2 * P], U8)
             copy(
                 out=grouped[:].rearrange("p t (a b) j -> p a j b t", b=2),

@@ -51,7 +51,7 @@ def tile_picked_edgeup_relu_p_kernel(
                 stop=stop,
             )
 
-        at_words0, at_words1, at_scales = 0, 4 * T, 8 * T
+        at_words0, at_words1, at_scales, at_reused = 0, 4 * T, 8 * T, 9 * T
         offsets = keep.tile([P, S // 16], U16, name="offsets", align_bytes=256)
         node_words = [placed("node_words0", [P, T], U32, at_words0), placed("node_words1", [P, T], U32, at_words1)]
         node_scales = placed("node_scales", [P, T], U8, at_scales)
@@ -72,12 +72,11 @@ def tile_picked_edgeup_relu_p_kernel(
             return raw
 
         nc.vector.memset(node_scales[:].bitcast(I32), 0)
-        for q in (0, 2, 3):
+        for q in range(4):
             load_node_scales(nc.gpsimd, q)
         nc.vector.memset(w4_plane[:].bitcast(I32), 0)
 
         load_words(node_words[0], x_words[0])
-        load_node_scales(nc.sync, 1)
         nc.sync.dma_start(offsets[:], offs)
         raw_w = [load_rows("raw_w0", w1[0:K_PASS, :], 0, H), load_rows("raw_w1", w2[0:K_PASS, :], 0, H)]
         load_words(node_words[1], x_words[1])
@@ -92,14 +91,15 @@ def tile_picked_edgeup_relu_p_kernel(
             )
 
         end_words = [tile("end_words0", [P, S], U32), tile("end_words1", [P, S], U32)]
-        end_scales = tile("end_scales", [P, S], U8)
         nc.vector.tensor_copy(end_words[0][:], node_words[0][:].indirect(offsets[:]))
-        nc.vector.tensor_copy(end_scales[:], node_scales[:].indirect(offsets[:]))
 
         hidden = [psum.tile([P, PACK, WIDTH], F32, name="hidden%d" % w) for w in range(len(WINDOWS))]
 
         def weight_half(n, u, copy):
-            grouped = tile("w_bf%d_%d" % (n, u), [P, 2, P, PACK], BF16)
+            if (n, u) == (0, 1):
+                grouped = placed("w_bf0_1", [P, 2, P, PACK], BF16, at_reused)
+            else:
+                grouped = tile("w_bf%d_%d" % (n, u), [P, 2, P, PACK], BF16)
             codes = tile("w_codes%d_%d" % (n, u), [P, 2 * P], U32)
             plane = tile("w_plane%d_%d" % (n, u), [P, 2 * P], U8)
             copy(
@@ -113,16 +113,26 @@ def tile_picked_edgeup_relu_p_kernel(
             cols = slice((t % 2) * P, (t % 2 + 1) * P)
             multiply(hidden[w][:, t, :], half[0][:, cols], half[1][:, cols], words, scales, start, stop)
 
+        first_halves = [weight_half(0, u, nc.scalar.copy) for u in range(2)]
+        end_scales = [placed("end_scales%d" % side, [P, V], U8, at_reused + side * V) for side in range(2)]
+        for side in range(2):
+            entries = offsets[:, side * V // 16 : (side + 1) * V // 16]
+            nc.vector.tensor_copy(end_scales[side][:], node_scales[:].indirect(entries))
+
         for n in range(4):
             z, side = divmod(n, 2)
             if n == 2:
                 nc.vector.tensor_copy(end_words[1][:], node_words[1][:].indirect(offsets[:]))
             for u in range(2):
-                half = weight_half(n, u, nc.vector.tensor_copy if (n == 3 and u == 0) else nc.scalar.copy)
+                if n == 0:
+                    half = first_halves[u]
+                else:
+                    half = weight_half(n, u, nc.vector.tensor_copy if (n == 3 and u == 0) else nc.scalar.copy)
                 for t in (2 * u, 2 * u + 1):
                     for w, (v0, count) in enumerate(WINDOWS):
-                        cols = slice(side * V + v0 + count - WIDTH, side * V + v0 + count)
-                        first_layer(w, t, half, end_words[z][:, cols], end_scales[4 * z : P, cols], n == 0 and t == 0, False)
+                        cols = slice(v0 + count - WIDTH, v0 + count)
+                        words = end_words[z][:, side * V : (side + 1) * V]
+                        first_layer(w, t, half, words[:, cols], end_scales[side][4 * z : P, cols], n == 0 and t == 0, False)
 
         w3_halves = [weight_half(4, 0, nc.vector.tensor_copy), weight_half(4, 1, nc.scalar.copy)]
 

@@ -72,11 +72,12 @@ def tile_picked_edgeup_relu_p_kernel(
             return raw
 
         nc.vector.memset(node_scales[:].bitcast(I32), 0)
-        for q in range(4):
+        for q in (0, 2, 3):
             load_node_scales(nc.gpsimd, q)
         nc.vector.memset(w4_plane[:].bitcast(I32), 0)
 
         load_words(node_words[0], x_words[0])
+        load_node_scales(nc.sync, 1)
         nc.sync.dma_start(offsets[:], offs)
         raw_w = [load_rows("raw_w0", w1[0:K_PASS, :], 0, H), load_rows("raw_w1", w2[0:K_PASS, :], 0, H)]
         load_words(node_words[1], x_words[1])

@@ -72,12 +72,15 @@ def tile_picked_edgeup_relu_p_kernel(
             return raw
 
         nc.vector.memset(node_scales[:].bitcast(I32), 0)
-        for q in (0, 2, 3):
+        for q in (0, 3):
             load_node_scales(nc.gpsimd, q)
         nc.vector.memset(w4_plane[:].bitcast(I32), 0)
 
         load_words(node_words[0], x_words[0])
-        load_node_scales(nc.sync, 1)
+        for z in range(2):
+            for q in (1, 2):
+                rows = slice(32 * q + 4 * z, 32 * q + 4 * z + 4)
+                nc.sync.dma_start(out=node_scales[rows, :].bitcast(I32), in_=x_scales[z, 4 * q : 4 * q + 4, :].bitcast(I32))
         nc.sync.dma_start(offsets[:], offs)
         raw_w = [load_rows("raw_w0", w1[0:K_PASS, :], 0, H), load_rows("raw_w1", w2[0:K_PASS, :], 0, H)]
         load_words(node_words[1], x_words[1])

@@ -17,6 +17,7 @@ RELU = mybir.ActivationFunctionType.Relu
 P = 128
 PACK = 4
 K_PASS = P * PACK
+QUADRANT = 32
 WIDTH = 128
 WINDOWS = [(0, 128), (128, 128), (256, 128), (384, 64), (448, 64)]
 PIECES = [(0, 256), (256, 384), (384, 512)]
@@ -51,17 +52,12 @@ def tile_picked_edgeup_relu_p_kernel(
                 stop=stop,
             )
 
-        at_words0, at_words1, at_scales, at_reused = 0, 4 * T, 8 * T, 9 * T
         offsets = keep.tile([P, S // 16], U16, name="offsets", align_bytes=256)
-        node_words = [placed("node_words0", [P, T], U32, at_words0), placed("node_words1", [P, T], U32, at_words1)]
+        at_words, at_scales = 0, 4 * T
+        node_words = [placed("node_words0", [P, T], U32, at_words), tile("node_words1", [P, T], U32)]
         node_scales = placed("node_scales", [P, T], U8, at_scales)
         w4_codes = tile("w4_codes", [P, N], U32)
         w4_plane = tile("w4_plane", [P, N], U8)
-
-        def load_node_scales(queue, q):
-            queue.dma_start(
-                out=node_scales[32 * q : 32 * q + 8, :].bitcast(I32), in_=x_scales[:, 4 * q : 4 * q + 4, :].bitcast(I32)
-            )
 
         def load_words(dst, words):
             nc.sync.dma_start(out=dst[:].bitcast(I32), in_=words.rearrange("p n t -> p (n t)").bitcast(I32))
@@ -72,17 +68,23 @@ def tile_picked_edgeup_relu_p_kernel(
             return raw
 
         nc.vector.memset(node_scales[:].bitcast(I32), 0)
-        for q in (0, 3):
-            load_node_scales(nc.gpsimd, q)
         nc.vector.memset(w4_plane[:].bitcast(I32), 0)
 
-        load_words(node_words[0], x_words[0])
-        for z in range(2):
-            for q in (1, 2):
-                rows = slice(32 * q + 4 * z, 32 * q + 4 * z + 4)
-                nc.sync.dma_start(out=node_scales[rows, :].bitcast(I32), in_=x_scales[z, 4 * q : 4 * q + 4, :].bitcast(I32))
+        raw_w = [load_rows("raw_w0", w1[0:K_PASS, :], 0, H)]
+        for q in (2, 3):
+            nc.gpsimd.dma_start(
+                out=node_scales[QUADRANT * q : QUADRANT * q + 8, :].bitcast(I32),
+                in_=x_scales[:, 4 * q : 4 * q + 4, :].bitcast(I32),
+            )
+        for q in (0, 1):
+            for z in range(2):
+                first = QUADRANT * q + 4 * z
+                nc.sync.dma_start(
+                    out=node_scales[first : first + 4, :].bitcast(I32), in_=x_scales[z, 4 * q : 4 * q + 4, :].bitcast(I32)
+                )
         nc.sync.dma_start(offsets[:], offs)
-        raw_w = [load_rows("raw_w0", w1[0:K_PASS, :], 0, H), load_rows("raw_w1", w2[0:K_PASS, :], 0, H)]
+        load_words(node_words[0], x_words[0])
+        raw_w.append(load_rows("raw_w1", w2[0:K_PASS, :], 0, H))
         load_words(node_words[1], x_words[1])
         raw_w.append(load_rows("raw_w2", w1[K_PASS:K, :], 0, H))
         raw_w.append(load_rows("raw_w3", w2[K_PASS:K, :], 0, H))
@@ -94,18 +96,19 @@ def tile_picked_edgeup_relu_p_kernel(
                 out=w4_plane[32 * q : 32 * q + 4, :].bitcast(I32), in_=w4_scales[0, 4 * q : 4 * q + 4, :].bitcast(I32)
             )
 
-        end_words = [tile("end_words0", [P, S], U32), tile("end_words1", [P, S], U32)]
-        nc.vector.tensor_copy(end_words[0][:], node_words[0][:].indirect(offsets[:]))
+        end_words = [tile("end_words0", [P, S], U32), placed("end_words1", [P, S], U32, at_scales + 4 * P)]
+        end_scales = [placed("end_scales%d" % side, [P, V], U8, at_words + side * V) for side in range(2)]
 
         hidden = [psum.tile([P, PACK, WIDTH], F32, name="hidden%d" % w) for w in range(len(WINDOWS))]
 
-        def weight_half(n, u, copy):
-            if (n, u) == (0, 1):
-                grouped = placed("w_bf0_1", [P, 2, P, PACK], BF16, at_reused)
-            else:
-                grouped = tile("w_bf%d_%d" % (n, u), [P, 2, P, PACK], BF16)
+        def weight_half(n, u):
+            grouped = tile("w_bf%d_%d" % (n, u), [P, 2, P, PACK], BF16)
             codes = tile("w_codes%d_%d" % (n, u), [P, 2 * P], U32)
-            plane = tile("w_plane%d_%d" % (n, u), [P, 2 * P], U8)
+            if n == 1:
+                plane = placed("w_plane1_%d" % u, [P, 2 * P], U8, at_scales + u * 2 * P)
+            else:
+                plane = tile("w_plane%d_%d" % (n, u), [P, 2 * P], U8)
+            copy = nc.vector.tensor_copy if u == 0 and n >= 3 else nc.scalar.copy
             copy(
                 out=grouped[:].rearrange("p t (a b) j -> p a j b t", b=2),
                 in_=raw_w[n][:].rearrange("p j (a b t) -> p a j b t", b=2, t=PACK)[:, :, :, :, 2 * u : 2 * u + 2],
@@ -117,28 +120,22 @@ def tile_picked_edgeup_relu_p_kernel(
             cols = slice((t % 2) * P, (t % 2 + 1) * P)
             multiply(hidden[w][:, t, :], half[0][:, cols], half[1][:, cols], words, scales, start, stop)
 
-        first_halves = [weight_half(0, u, nc.scalar.copy) for u in range(2)]
-        end_scales = [placed("end_scales%d" % side, [P, V], U8, at_reused + side * V) for side in range(2)]
-        for side in range(2):
-            entries = offsets[:, side * V // 16 : (side + 1) * V // 16]
-            nc.vector.tensor_copy(end_scales[side][:], node_scales[:].indirect(entries))
-
         for n in range(4):
             z, side = divmod(n, 2)
-            if n == 2:
-                nc.vector.tensor_copy(end_words[1][:], node_words[1][:].indirect(offsets[:]))
+            if side == 0:
+                nc.vector.tensor_copy(end_words[z][:], node_words[z][:].indirect(offsets[:]))
+            if z == 0:
+                entries = offsets[:, side * V // 16 : (side + 1) * V // 16]
+                nc.vector.tensor_copy(end_scales[side][:], node_scales[:].indirect(entries))
             for u in range(2):
-                if n == 0:
-                    half = first_halves[u]
-                else:
-                    half = weight_half(n, u, nc.vector.tensor_copy if (n == 3 and u == 0) else nc.scalar.copy)
+                half = weight_half(n, u)
                 for t in (2 * u, 2 * u + 1):
                     for w, (v0, count) in enumerate(WINDOWS):
                         cols = slice(v0 + count - WIDTH, v0 + count)
                         words = end_words[z][:, side * V : (side + 1) * V]
                         first_layer(w, t, half, words[:, cols], end_scales[side][4 * z : P, cols], n == 0 and t == 0, False)
 
-        w3_halves = [weight_half(4, 0, nc.vector.tensor_copy), weight_half(4, 1, nc.scalar.copy)]
+        w3_halves = [weight_half(4, u) for u in range(2)]
 
         e_codes = {0: tile("e_codes0", [P, WIDTH], U32), 2: tile("e_codes2", [P, WIDTH], U32)}
         e_plane = {0: tile("e_plane0", [P, WIDTH], U8), 2: tile("e_plane2", [P, WIDTH], U8)}

@@ -71,13 +71,13 @@ def tile_picked_edgeup_relu_p_kernel(
         nc.vector.memset(w4_plane[:].bitcast(I32), 0)
 
         raw_w = [load_rows("raw_w0", w1[0:K_PASS, :], 0, H)]
-        for q in (2, 3):
+        for q in (0, 3):
             nc.gpsimd.dma_start(
                 out=node_scales[QUADRANT * q : QUADRANT * q + 8, :].bitcast(I32),
                 in_=x_scales[:, 4 * q : 4 * q + 4, :].bitcast(I32),
             )
-        for q in (0, 1):
-            for z in range(2):
+        for z in range(2):
+            for q in (1, 2):
                 first = QUADRANT * q + 4 * z
                 nc.sync.dma_start(
                     out=node_scales[first : first + 4, :].bitcast(I32), in_=x_scales[z, 4 * q : 4 * q + 4, :].bitcast(I32)

@@ -68,7 +68,6 @@ def tile_picked_edgeup_relu_p_kernel(
             return raw
 
         nc.vector.memset(node_scales[:].bitcast(I32), 0)
-        nc.vector.memset(w4_plane[:].bitcast(I32), 0)
 
         raw_w = [load_rows("raw_w0", w1[0:K_PASS, :], 0, H)]
         for q in (0, 3):

from contextlib import ExitStack

import concourse.mybir as mybir

K, T, S, V, H, N, J = 1024, 2048, 1024, 512, 512, 128, 512
FLOPS = 2 * V * H * (2 * K + J) + 2 * V * H * N

F32 = mybir.dt.float32
BF16 = mybir.dt.bfloat16
I32 = mybir.dt.int32
U32 = mybir.dt.uint32
U16 = mybir.dt.uint16
U8 = mybir.dt.uint8
FP8X4 = mybir.dt.float8_e4m3fn_x4
RELU = mybir.ActivationFunctionType.Relu

P = 128
PACK = 4
K_PASS = P * PACK
QUADRANT = 32
WIDTH = 128
WINDOWS = [(0, 128), (128, 128), (256, 128), (384, 64), (448, 64)]
PIECES = [(0, 256), (256, 384), (384, 512)]


def tile_picked_edgeup_relu_p_kernel(
    tc, x_words, x_scales, eT, w1, w2, w3, w4_words, w4_scales, offs, out
):
    nc = tc.nc
    with ExitStack() as ctx:
        keep = ctx.enter_context(tc.tile_pool(name="keep", bufs=1))
        chain = ctx.enter_context(tc.tile_pool(name="chain", bufs=1))
        psum = ctx.enter_context(tc.psum_pool(name="psum", bufs=1))

        def tile(name, shape, dtype):
            return keep.tile(shape, dtype, name=name, align_bytes=256)

        def placed(name, shape, dtype, offset):
            return chain.tile(shape, dtype, name=name, align_bytes=256, offset=offset)

        def quantize(codes, plane, rounded):
            nc.vector.quantize_mx(out=codes.bitcast(FP8X4), scales=plane, in_=rounded)

        def multiply(sums, still, still_plane, moving, moving_plane, start, stop):
            nc.tensor.matmul_mx(
                out=sums,
                lhsT=still.bitcast(FP8X4),
                lhsT_scale=still_plane,
                rhs=moving.bitcast(FP8X4),
                rhs_scale=moving_plane,
                start=start,
                stop=stop,
            )

        offsets = keep.tile([P, S // 16], U16, name="offsets", align_bytes=256)
        at_words, at_scales = 0, 4 * T
        node_words = [placed("node_words0", [P, T], U32, at_words), tile("node_words1", [P, T], U32)]
        node_scales = placed("node_scales", [P, T], U8, at_scales)
        w4_codes = tile("w4_codes", [P, N], U32)
        w4_plane = tile("w4_plane", [P, N], U8)

        def load_words(dst, words):
            nc.sync.dma_start(out=dst[:].bitcast(I32), in_=words.rearrange("p n t -> p (n t)").bitcast(I32))

        def load_rows(name, rows, c0, c1):
            raw = tile(name, [P, PACK, c1 - c0], F32)
            nc.sync.dma_start(out=raw[:], in_=rows.rearrange("(p j) c -> p j c", j=PACK)[:, :, c0:c1])
            return raw

        nc.vector.memset(node_scales[:].bitcast(I32), 0)

        raw_w = [load_rows("raw_w0", w1[0:K_PASS, :], 0, H)]
        for q in (0, 3):
            nc.gpsimd.dma_start(
                out=node_scales[QUADRANT * q : QUADRANT * q + 8, :].bitcast(I32),
                in_=x_scales[:, 4 * q : 4 * q + 4, :].bitcast(I32),
            )
        for z in range(2):
            for q in (1, 2):
                first = QUADRANT * q + 4 * z
                nc.sync.dma_start(
                    out=node_scales[first : first + 4, :].bitcast(I32), in_=x_scales[z, 4 * q : 4 * q + 4, :].bitcast(I32)
                )
        nc.sync.dma_start(offsets[:], offs)
        load_words(node_words[0], x_words[0])
        raw_w.append(load_rows("raw_w1", w2[0:K_PASS, :], 0, H))
        load_words(node_words[1], x_words[1])
        raw_w.append(load_rows("raw_w2", w1[K_PASS:K, :], 0, H))
        raw_w.append(load_rows("raw_w3", w2[K_PASS:K, :], 0, H))
        raw_w.append(load_rows("raw_w4", w3, 0, H))
        raw_e = [load_rows("raw_e%d" % n, eT, c0, c1) for n, (c0, c1) in enumerate(PIECES)]
        load_words(w4_codes, w4_words[0])
        for q in range(4):
            nc.sync.dma_start(
                out=w4_plane[32 * q : 32 * q + 4, :].bitcast(I32), in_=w4_scales[0, 4 * q : 4 * q + 4, :].bitcast(I32)
            )

        end_words = [tile("end_words0", [P, S], U32), placed("end_words1", [P, S], U32, at_scales + 4 * P)]
        end_scales = [placed("end_scales%d" % side, [P, V], U8, at_words + side * V) for side in range(2)]

        hidden = [psum.tile([P, PACK, WIDTH], F32, name="hidden%d" % w) for w in range(len(WINDOWS))]

        def weight_half(n, u):
            grouped = tile("w_bf%d_%d" % (n, u), [P, 2, P, PACK], BF16)
            codes = tile("w_codes%d_%d" % (n, u), [P, 2 * P], U32)
            if n == 1:
                plane = placed("w_plane1_%d" % u, [P, 2 * P], U8, at_scales + u * 2 * P)
            else:
                plane = tile("w_plane%d_%d" % (n, u), [P, 2 * P], U8)
            copy = nc.vector.tensor_copy if u == 0 and n >= 3 else nc.scalar.copy
            copy(
                out=grouped[:].rearrange("p t (a b) j -> p a j b t", b=2),
                in_=raw_w[n][:].rearrange("p j (a b t) -> p a j b t", b=2, t=PACK)[:, :, :, :, 2 * u : 2 * u + 2],
            )
            quantize(codes[:], plane[:], grouped[:].rearrange("p t m j -> p (t m j)"))
            return codes, plane

        def first_layer(w, t, half, words, scales, start, stop):
            cols = slice((t % 2) * P, (t % 2 + 1) * P)
            multiply(hidden[w][:, t, :], half[0][:, cols], half[1][:, cols], words, scales, start, stop)

        for n in range(4):
            z, side = divmod(n, 2)
            if side == 0:
                nc.vector.tensor_copy(end_words[z][:], node_words[z][:].indirect(offsets[:]))
            if z == 0:
                entries = offsets[:, side * V // 16 : (side + 1) * V // 16]
                nc.vector.tensor_copy(end_scales[side][:], node_scales[:].indirect(entries))
            for u in range(2):
                half = weight_half(n, u)
                for t in (2 * u, 2 * u + 1):
                    for w, (v0, count) in enumerate(WINDOWS):
                        cols = slice(v0 + count - WIDTH, v0 + count)
                        words = end_words[z][:, side * V : (side + 1) * V]
                        first_layer(w, t, half, words[:, cols], end_scales[side][4 * z : P, cols], n == 0 and t == 0, False)

        w3_halves = [weight_half(4, u) for u in range(2)]

        e_codes = {0: tile("e_codes0", [P, WIDTH], U32), 2: tile("e_codes2", [P, WIDTH], U32)}
        e_plane = {0: tile("e_plane0", [P, WIDTH], U8), 2: tile("e_plane2", [P, WIDTH], U8)}
        row_codes = tile("e_row_codes", [P, 2 * WIDTH], U32)
        row_plane = tile("e_row_plane", [P, 2 * WIDTH], U8)
        row_end = {1: 128, 3: 192, 4: 256}

        def edge_columns(w, count):
            if w in row_end:
                cols = slice(row_end[w] - count, row_end[w])
                return row_codes[:, cols], row_plane[:, cols]
            return e_codes[w][:], e_plane[w][:]

        def round_edges(w, copy):
            v0, count = WINDOWS[w]
            n = [c0 <= v0 < c1 for c0, c1 in PIECES].index(True)
            at = v0 - PIECES[n][0]
            e_bf = keep.tile([P, count, PACK], BF16, name="e_bf%d" % w, tag={3: "e_bf2", 4: "h_bf2"}.get(w, "e_bf%d" % w), align_bytes=256)
            copy(
                out=e_bf[:].rearrange("p (c i) j -> p c j i", i=4),
                in_=raw_e[n][:, :, at : at + count].rearrange("p j (c i) -> p c j i", i=4),
            )
            return e_bf

        def close_window(w, e_bf):
            quantize(*edge_columns(w, WINDOWS[w][1]), e_bf[:].rearrange("p c j -> p (c j)"))
            for t in range(PACK):
                first_layer(w, t, w3_halves[t // 2], *edge_columns(w, WIDTH), False, t == PACK - 1)

        def relu(w, on_vector):
            count = WINDOWS[w][1]
            h_bf = tile("h_bf%d" % w, [P, count, PACK], BF16)
            sums = hidden[w][:, :, WIDTH - count : WIDTH].rearrange("p t v -> p v t")
            if on_vector:
                nc.vector.tensor_scalar_max(h_bf[:], sums, 0.0)
            else:
                nc.scalar.activation(out=h_bf[:], in_=sums, func=RELU)
            return h_bf

        spare = [psum.tile([P, WIDTH], F32, name="acc%d" % n) for n in range(3)]
        acc = [spare[0][:], spare[1][:], hidden[0][:, 0, :], spare[2][:, 0:64], hidden[1][:, 0, 0:64]]
        results = [tile("result%d" % c, [P, WIDTH], F32) for c in range(V // WIDTH)]

        def second_layer(w, h_bf):
            count = WINDOWS[w][1]
            h_codes = tile("h_codes%d" % w, [P, count], U32)
            h_plane = tile("h_plane%d" % w, [P, count], U8)
            quantize(h_codes[:], h_plane[:], h_bf[:].rearrange("p v t -> p (v t)"))
            multiply(acc[w], w4_codes[:], w4_plane[:], h_codes[:], h_plane[:], True, True)

        def leave(w, copy):
            v0, count = WINDOWS[w]
            c, at = divmod(v0, WIDTH)
            copy(out=results[c][:, at : at + count], in_=acc[w])
            if at + count == WIDTH:
                nc.sync.dma_start(out=out[:, c * WIDTH : (c + 1) * WIDTH], in_=results[c][:])

        for w, copy in ((0, nc.scalar.copy), (1, nc.vector.tensor_copy), (2, nc.scalar.copy)):
            close_window(w, round_edges(w, copy))
        narrow = [round_edges(w, nc.vector.tensor_copy) for w in (3, 4)]
        close_window(3, narrow[0])
        close_window(4, narrow[1])
        rounded = [relu(w, w == 2) for w in range(len(WINDOWS))]
        for w in range(len(WINDOWS)):
            second_layer(w, rounded[w])
        for w in range(len(WINDOWS)):
            leave(w, nc.scalar.copy if w < 3 else nc.vector.tensor_copy)
